import numpy as np
import ml_dtypes


def mxq(x, axis, fmt="e4m3"):
    dtype, down = {"e4m3": (ml_dtypes.float8_e4m3fn, 7), "e5m2": (ml_dtypes.float8_e5m2, 14)}[fmt]
    v = np.moveaxis(np.asarray(x, np.float32).astype(ml_dtypes.bfloat16).astype(np.float64), axis, -1)
    blocks = v.reshape(v.shape[:-1] + (-1, 32))
    amax = np.abs(blocks).max(-1, keepdims=True)
    byte = np.maximum(np.where(amax > 0, np.frexp(amax)[1] - 1 + 127, 0) - down, 1)
    scale = np.exp2(byte - 127.0)
    codes = (blocks / scale).astype(np.float32).astype(dtype).astype(np.float64)
    return np.moveaxis((codes * scale).reshape(v.shape), -1, axis)


WIDE = False


def mx_kscale(k):
    if not WIDE:
        return np.ones(k)
    levels = np.array([10, -10, 5, -5, 0])
    if k % 512:
        return np.exp2(np.random.permutation(np.resize(levels, k // 32))).repeat(32)
    a = np.empty((k // 512, 16))
    for p in range(k // 512):
        a[p, :8] = np.random.permutation(np.resize(levels, 8))
        for g in range(8):
            far = levels[np.abs(levels - a[p, g]) >= 10]
            a[p, g + 8] = far[np.random.randint(len(far))]
    return np.exp2(a.ravel()).repeat(32)


def f64(x):
    return np.asarray(x).astype(np.float64)


def striped(idx):
    return np.tile(idx.reshape(-1, 16).T, (8, 1)).astype(np.uint16)


def unstriped(offs):
    return offs[:16].T.reshape(-1).astype(np.int64)


def striped8(idx):
    return np.concatenate([x.reshape(-1, 16).T for x in idx]).astype(np.uint16)


def runs(offs, k):
    lists = np.stack([offs[16 * r : 16 * r + 16].T.reshape(-1) for r in range(8)]).astype(np.int64)
    return lists[np.arange(k) % 512 // 64]


def pack_weight(w):
    k, n = w.shape
    w = f64(np.asarray(w, np.float32).astype(ml_dtypes.bfloat16)).reshape(k // 32, 32, n)
    amax = np.abs(w).max(1)
    byte = np.clip(np.where(amax > 0, np.frexp(amax)[1] - 1 + 127 - 7, 1), 1, 254)
    scaled = (w * np.exp2(127.0 - byte)[:, None, :]).reshape(k, n).astype(np.float32)
    words = np.ascontiguousarray(scaled.reshape(k // 512, 128, 4, n).transpose(0, 1, 3, 2)).astype(ml_dtypes.float8_e4m3fn).view(np.uint8)
    return words, np.ascontiguousarray(byte.astype(np.uint8).reshape(k // 512, 16, n))


def unpack_weight(words, scales):
    g, p, n, _ = words.shape
    vals = np.ascontiguousarray(words).view(ml_dtypes.float8_e4m3fn).astype(np.float64) * np.repeat(np.exp2(scales.astype(np.float64) - 127.0), 8, axis=1)[..., None]
    return vals.transpose(0, 1, 3, 2).reshape(g * 512, n)


E2M1 = np.array([0.0, 0.5, 1.0, 1.5, 2.0, 3.0, 4.0, 6.0, -0.0, -0.5, -1.0, -1.5, -2.0, -3.0, -4.0, -6.0])


def pack_fp4(w):
    k, n = w.shape
    w = f64(np.asarray(w, np.float32).astype(ml_dtypes.bfloat16)).reshape(k // 32, 32, n)
    amax = np.abs(w).max(1)
    mant, ex = np.frexp(amax / 6.0)
    byte = np.clip(np.where(amax > 0, np.where(mant > 0.5, ex, ex - 1) + 127, 1), 1, 254)
    scaled = (w * np.exp2(127.0 - byte)[:, None, :]).reshape(k, n).astype(np.float32)
    c = np.ascontiguousarray(scaled.reshape(k // 512, 128, 4, n).transpose(0, 1, 3, 2)).astype(ml_dtypes.float4_e2m1fn).view(np.uint8) & 0xF
    words = (c[..., 0::2] | (c[..., 1::2] << 4)).reshape(k // 512, 128, 2 * n)
    return np.ascontiguousarray(words), np.ascontiguousarray(byte.astype(np.uint8).reshape(k // 512, 16, n))


def unpack_fp4(words, scales):
    g, _, n = scales.shape
    words = np.ascontiguousarray(words).reshape(g, 128, n, 2)
    nib = np.empty((g, 128, n, 4), np.uint8)
    nib[..., 0::2] = words & 0xF
    nib[..., 1::2] = words >> 4
    vals = E2M1[nib] * np.repeat(np.exp2(scales.astype(np.float64) - 127.0), 8, axis=1)[..., None]
    return vals.transpose(0, 1, 3, 2).reshape(g * 512, n)


def planes(y):
    n, m = y.shape
    v = y.astype(np.float32).astype(ml_dtypes.bfloat16).astype(np.float64).reshape(n // 32, 32, m)
    top = np.abs(v).max(1)
    byte = np.clip(np.where(top > 0, np.frexp(top)[1] - 1 + 127 - 7, 1), 1, 254)
    codes = (v * np.exp2(127.0 - byte)[:, None, :]).reshape(n, m).astype(np.float32).astype(ml_dtypes.float8_e4m3fn).view(np.uint8)
    words = codes.reshape(n // 512, 128, 4, m).transpose(0, 1, 3, 2)
    return np.ascontiguousarray(words), np.ascontiguousarray(byte.astype(np.uint8).reshape(n // 512, 16, m))


K, T, S, N, G, H, W = 512, 2048, 512, 512, 2048, 512, 256


def setup_inputs():
    n = np.random.standard_normal
    s = mx_kscale(K)[:, None]
    u = mx_kscale(S)
    packed_xT = pack_weight(n((K, T)) * s)
    packed_dT = pack_weight(n((K, G)) / s)
    packed_w1 = pack_fp4(n((H, N)) / np.sqrt(H) / u[:, None])
    perm = np.stack([np.random.permutation(S) for _ in range(8)])
    return {
        "x_words": packed_xT[0],
        "x_scales": packed_xT[1],
        "d_words": packed_dT[0],
        "d_scales": packed_dT[1],
        "gn": (np.random.uniform(0.5, 1.5, (H, 1)) * u[:, None]).astype(np.float32),
        "w1_words": packed_w1[0],
        "w1_scales": packed_w1[1],
        "offs": striped(np.random.permutation(T)[:S]),
        "kidx": striped8(np.random.randint(0, G, (8, H))),
        "n1": striped8(np.stack([np.random.permutation(S) for _ in range(8)])),
        "n2": striped8(np.stack([np.random.permutation(S) for _ in range(8)])),
        "n3": striped8(perm[:, :W]),
        "n4": striped8(perm[:, W:]),
    }


def reference(x_words, x_scales, d_words, d_scales, gn, w1_words, w1_scales, offs, kidx, n1, n2, n3, n4):
    d_kidx = unpack_weight(d_words, d_scales)[np.arange(K)[:, None], runs(kidx, K)]
    xq = unpack_weight(x_words, x_scales)[:, unstriped(offs)]
    s = 0.0625 * (d_kidx.T @ xq)
    z = f64(gn) * (0.75 * ((s - (s[np.arange(H)[:, None], runs(n1, H)])) * (s - (s[np.arange(H)[:, None], runs(n2, H)]))))
    h = unpack_fp4(w1_words, w1_scales).T @ mxq(z, 0, "e4m3")
    pa = h[np.arange(N)[:, None], runs(n3, N)]
    pb = h[np.arange(N)[:, None], runs(n4, N)]
    rb = pa * pb
    ra = pa + pb
    ds = np.zeros((N, S))
    ds[np.arange(N)[:, None], runs(n3, N)] = ra
    out = ds.copy()
    out[np.arange(N)[:, None], runs(n4, N)] = rb
    return (out,) + planes(out)

@@ -1,0 +1,231 @@
+from contextlib import ExitStack
+
+import concourse.mybir as mybir
+
+FLOPS = 536870912
+
+F32 = mybir.dt.float32
+BF16 = mybir.dt.bfloat16
+I32 = mybir.dt.int32
+U32 = mybir.dt.uint32
+U16 = mybir.dt.uint16
+U8 = mybir.dt.uint8
+FP8X4 = mybir.dt.float8_e4m3fn_x4
+FP4X4 = mybir.dt.float4_e2m1fn_x4
+ALU = mybir.AluOpType
+COPY = mybir.ActivationFunctionType.Copy
+
+P = 128
+PACK = 4
+TABLE = 2048
+S = 512
+HALF = S // 2
+Z_FACTOR = 0.75 * 0.0625 * 0.0625
+
+
+def tile_picked_keyquadbond_none_po_kernel(
+    tc, x_words, x_scales, d_words, d_scales, gn, w1_words, w1_scales, offs, kidx, n1, n2, n3, n4, out_0, out_1, out_2
+):
+    nc = tc.nc
+    with ExitStack() as ctx:
+        lists = ctx.enter_context(tc.tile_pool(name="lists", bufs=1))
+        sb = ctx.enter_context(tc.tile_pool(name="sb", bufs=1))
+        ps = ctx.enter_context(tc.psum_pool(name="ps", bufs=1))
+
+        def load_list(name, dram):
+            t = lists.tile(list(dram.shape), U16, name=name)
+            nc.sync.dma_start(t[:], dram)
+            return t
+
+        def load_scale_table(name, dram):
+            width = dram.shape[2]
+            t = sb.tile([P, width], U8, name=name, align_bytes=64)
+            rows = dram[0].bitcast(I32).unsqueeze(1).to_broadcast([16, 8, width // 4])
+            nc.sync.dma_start(t[:].bitcast(I32), rows)
+            return t
+
+        def load_word_table(name, dram):
+            t = sb.tile([P, TABLE], I32, name=name, align_bytes=64)
+            nc.sync.dma_start(t[:], dram[0].rearrange("p n t -> p (n t)").bitcast(I32))
+            return t
+
+        kidx_sb = load_list("kidx_sb", kidx)
+        d_byte_table = load_scale_table("d_byte_table", d_scales)
+        offs_sb = load_list("offs_sb", offs)
+        x_byte_table = load_scale_table("x_byte_table", x_scales)
+        n1_sb = load_list("n1_sb", n1)
+        n2_sb = load_list("n2_sb", n2)
+        d_word_table = load_word_table("d_word_table", d_words)
+        x_word_table = load_word_table("x_word_table", x_words)
+        w_raw = sb.tile([P, 2 * S], U8, name="w_raw", align_bytes=64)
+        nc.sync.dma_start(w_raw[:].bitcast(I32), w1_words[0].bitcast(I32))
+        w_bytes_raw = load_scale_table("w_bytes_raw", w1_scales)
+        n3_sb = load_list("n3_sb", n3)
+        n4_sb = load_list("n4_sb", n4)
+
+        gn_sb = sb.tile([P, PACK], F32, name="gn_sb")
+        nc.gpsimd.dma_start(gn_sb[:], gn.rearrange("(p t) o -> p (t o)", t=PACK))
+        key_weight = sb.tile([P, PACK], F32, name="key_weight")
+        nc.scalar.activation(key_weight[:], gn_sb[:], COPY, scale=Z_FACTOR)
+
+        d_bytes_picked = sb.tile([P, S], U8, name="d_bytes_picked", align_bytes=64)
+        x_bytes_picked = sb.tile([P, S], U8, name="x_bytes_picked", align_bytes=64)
+        planes = sb.tile([P, 2 * S], U8, name="planes", align_bytes=64)
+        nc.vector.tensor_copy(d_bytes_picked[:], d_byte_table[:].indirect(kidx_sb[:]))
+        nc.vector.tensor_copy(x_bytes_picked[:], x_byte_table[:].indirect(offs_sb[:]))
+        nc.vector.tensor_copy(
+            planes[:, :S].rearrange("p (t m) -> p t m", t=PACK), d_bytes_picked[:].rearrange("p (m t) -> p t m", t=PACK)
+        )
+        nc.vector.tensor_copy(planes[:, S:].bitcast(I32), x_bytes_picked[:].bitcast(I32))
+        for r in range(1, 4):
+            nc.scalar.dma_start(planes[r:P:32, :].bitcast(I32), planes[8 * r : P : 32, :].bitcast(I32))
+        d_plane = planes[:, :S]
+        x_plane = planes[:, S:]
+
+        d_picked = sb.tile([P, S], I32, name="d_picked", align_bytes=64)
+        d_dealt = sb.tile([P, S], I32, name="d_dealt", align_bytes=64)
+        nc.vector.tensor_copy(d_picked[:].bitcast(U32), d_word_table[:].bitcast(U32).indirect(kidx_sb[:]))
+        x_picked = [sb.tile([P, HALF], I32, name="x_picked%d" % a, align_bytes=64) for a in range(2)]
+        nc.vector.tensor_copy(
+            d_dealt[:].rearrange("p (t m) -> p t m", t=PACK), d_picked[:].rearrange("p (m t) -> p t m", t=PACK)
+        )
+        for a in range(2):
+            nc.vector.tensor_copy(x_picked[a][:].bitcast(U32), x_word_table[:].bitcast(U32).indirect(offs_sb[:, 16 * a : 16 * a + 16]))
+
+        w_dealt = sb.tile([P, 2 * S], U8, name="w_dealt", align_bytes=64)
+        w_plane = sb.tile([P, S], U8, name="w_plane", align_bytes=64)
+        nc.vector.tensor_copy(
+            w_dealt[:].rearrange("p (t m b) -> p t m b", t=PACK, b=2), w_raw[:].rearrange("p (m t b) -> p t m b", t=PACK, b=2)
+        )
+        nc.vector.tensor_copy(
+            w_plane[:].rearrange("p (t m) -> p t m", t=PACK), w_bytes_raw[:].rearrange("p (m t) -> p t m", t=PACK)
+        )
+        for r in range(1, 4):
+            nc.sync.dma_start(w_plane[r:P:32, :].bitcast(I32), w_plane[8 * r : P : 32, :].bitcast(I32))
+
+        banks = [ps.tile([P, S], F32, name="bank%d" % b) for b in range(8)]
+        window = [sb.tile([P, S if t == 0 else 2 * S], F32, name="window%d" % t) for t in range(PACK)]
+        last_plain = sb.tile([P, S], F32, name="last_plain")
+        plain = [window[t + 1][:, S:] for t in range(PACK - 1)] + [last_plain[:]]
+        diff1 = sb.tile([P, PACK, S], F32, name="diff1")
+        diff1w = sb.tile([P, PACK, S], F32, name="diff1w")
+        diff2 = sb.tile([P, PACK, S], F32, name="diff2")
+
+        def score(t, a):
+            cols = slice(HALF * a, HALF * (a + 1))
+            bank = banks[2 * t + a][:, :HALF]
+            nc.tensor.matmul_mx(
+                bank,
+                lhsT=d_dealt[:, P * t : P * (t + 1)].bitcast(FP8X4),
+                lhsT_scale=d_plane[:, P * t : P * (t + 1)],
+                rhs=x_picked[a][:].bitcast(FP8X4),
+                rhs_scale=x_plane[:, cols],
+                start=True,
+                stop=True,
+            )
+            nc.scalar.copy(window[t][:, cols], bank)
+            nc.scalar.copy(plain[t][:, cols], bank)
+
+        def differences(t, cols):
+            lcols = slice(cols.start // 16, cols.stop // 16)
+            nc.vector.tensor_tensor(diff1[:, t, cols], window[t][:].indirect(n1_sb[:, lcols]), plain[t][:, cols], ALU.subtract)
+            nc.vector.tensor_tensor(diff2[:, t, cols], window[t][:].indirect(n2_sb[:, lcols]), plain[t][:, cols], ALU.subtract)
+
+        for t in range(PACK):
+            score(t, 0)
+            score(t, 1)
+        for t in range(PACK):
+            if t == 0:
+                differences(t, slice(0, HALF))
+                differences(t, slice(HALF, S))
+            else:
+                differences(t, slice(0, S))
+            nc.scalar.activation(diff1w[:, t, :], diff1[:, t, :], COPY, scale=key_weight[:, t : t + 1])
+
+        z = sb.tile([P, S, PACK], BF16, name="z", align_bytes=64)
+        z_codes = sb.tile([P, S], U32, name="z_codes", align_bytes=64)
+        z_plane = sb.tile([P, S], U8, name="z_plane", align_bytes=64)
+        h = [sb.tile([P, S], F32, name="h%d" % t) for t in range(PACK)]
+
+        def product(cols):
+            nc.vector.tensor_tensor(
+                z[:, cols, :].rearrange("p (c i) t -> p c t i", i=4),
+                diff1w[:, :, cols].rearrange("p t (c i) -> p c t i", i=4),
+                diff2[:, :, cols].rearrange("p t (c i) -> p c t i", i=4),
+                ALU.mult,
+            )
+
+        def quantise_z(cols):
+            nc.vector.quantize_mx(z_codes[:, cols].bitcast(FP8X4), z_plane[:, cols], z[:, cols, :].rearrange("p c t -> p (c t)"))
+
+        def values(t, cols, bank):
+            nc.tensor.matmul_mx(
+                bank[:, cols],
+                lhsT=w_dealt[:, 2 * P * t : 2 * P * (t + 1)].bitcast(FP4X4),
+                lhsT_scale=w_plane[:, P * t : P * (t + 1)],
+                rhs=z_codes[:, cols].bitcast(FP8X4),
+                rhs_scale=z_plane[:, cols],
+                start=True,
+                stop=True,
+            )
+            nc.scalar.copy(h[t][:, cols], bank[:, cols])
+
+        chunks = [slice(0, 256), slice(256, 384), slice(384, 512)]
+        product(chunks[0])
+        product(chunks[1])
+        quantise_z(chunks[0])
+        values(0, chunks[0], banks[0])
+        product(chunks[2])
+        quantise_z(chunks[1])
+        values(0, chunks[1], banks[1])
+        quantise_z(chunks[2])
+        values(0, chunks[2], banks[2])
+        for t in range(1, PACK):
+            values(t, slice(0, S), banks[2 + t])
+
+        pa = [sb.tile([P, HALF], F32, name="pa%d" % t) for t in range(PACK)]
+        pb = [sb.tile([P, HALF], F32, name="pb%d" % t) for t in range(PACK)]
+        y = [sb.tile([P, S], F32, name="y%d" % t) for t in range(PACK)]
+        y_grouped = sb.tile([P, S, PACK], BF16, name="y_grouped", align_bytes=64)
+        y_codes = sb.tile([P, S], I32, name="y_codes", align_bytes=64)
+        y_plane = sb.tile([P, S], U8, name="y_plane", align_bytes=64)
+        out_rows = out_0.rearrange("(p t) j -> p t j", t=PACK)
+
+        def fetch_a(t):
+            nc.vector.tensor_copy(pa[t][:], h[t][:].indirect(n3_sb[:]))
+
+        def fetch_b(t):
+            nc.vector.tensor_copy(pb[t][:], h[t][:].indirect(n4_sb[:]))
+
+        def put_sum(t):
+            nc.vector.tensor_tensor(y[t][:].indirect(n3_sb[:]), pa[t][:], pb[t][:], ALU.add)
+
+        def put_product(t):
+            nc.vector.tensor_tensor(y[t][:].indirect(n4_sb[:]), pa[t][:], pb[t][:], ALU.mult)
+            nc.sync.dma_start(out_rows[:, t, :], y[t][:])
+
+        fetch_a(0)
+        fetch_b(0)
+        for t in range(PACK):
+            if t + 1 < PACK:
+                fetch_a(t + 1)
+            put_sum(t)
+            if t + 1 < PACK:
+                fetch_b(t + 1)
+            put_product(t)
+            if t < 2:
+                nc.scalar.copy(y_grouped[:, :, t], y[t][:])
+            elif t == 2:
+                nc.scalar.copy(y_grouped[:, :, 2:4], y[t][:].unsqueeze(2).to_broadcast([P, S, 2]))
+        nc.vector.tensor_copy(y_grouped[:, :256, 3], y[3][:, :256])
+        nc.vector.tensor_copy(y_grouped[:, 256:384, 3], y[3][:, 256:384])
+        nc.scalar.copy(y_grouped[:, 384:, 3], y[3][:, 384:])
+        words_out = out_1[0].rearrange("p n t -> p (n t)").bitcast(I32)
+        for a in range(2):
+            cols = slice(HALF * a, HALF * (a + 1))
+            nc.vector.quantize_mx(y_codes[:, cols].bitcast(FP8X4), y_plane[:, cols], y_grouped[:, cols, :].rearrange("p c t -> p (c t)"))
+            queue = nc.sync if a == 0 else nc.scalar
+            queue.dma_start(words_out[:, cols], y_codes[:, cols])
+        for q in range(4):
+            queue = nc.sync if q % 2 == 0 else nc.scalar
+            queue.dma_start(out_2[0, 4 * q : 4 * q + 4, :].bitcast(I32), y_plane[32 * q : 32 * q + 4, :].bitcast(I32))

@@ -37,11 +37,11 @@ def tile_picked_keyquadbond_none_po_kernel(
             nc.sync.dma_start(t[:], dram)
             return t
 
-        def load_scale_table(name, dram):
+        def load_scale_table(name, dram, tag):
             width = dram.shape[2]
-            t = sb.tile([P, width], U8, name=name, align_bytes=64)
-            rows = dram[0].bitcast(I32).unsqueeze(1).to_broadcast([16, 8, width // 4])
-            nc.sync.dma_start(t[:].bitcast(I32), rows)
+            t = sb.tile([P, width], U8, name=name, tag=tag, align_bytes=64)
+            nc.gpsimd.memset(t[:].bitcast(I32), 0)
+            nc.sync.dma_start(t[0:P:8, :].bitcast(I32), dram[0].bitcast(I32))
             return t
 
         def load_word_table(name, dram):
@@ -50,26 +50,26 @@ def tile_picked_keyquadbond_none_po_kernel(
             return t
 
         kidx_sb = load_list("kidx_sb", kidx)
-        d_byte_table = load_scale_table("d_byte_table", d_scales)
+        d_byte_table = sb.tile([P, TABLE], U8, name="d_byte_table", align_bytes=64)
+        nc.sync.dma_start(d_byte_table[:].bitcast(I32), d_scales[0].bitcast(I32).unsqueeze(1).to_broadcast([16, 8, TABLE // 4]))
         offs_sb = load_list("offs_sb", offs)
-        x_byte_table = load_scale_table("x_byte_table", x_scales)
+        gn_sb = sb.tile([P, PACK], F32, name="gn_sb")
+        nc.sync.dma_start(gn_sb[:], gn.rearrange("(p t) o -> p (t o)", t=PACK))
         n1_sb = load_list("n1_sb", n1)
-        n2_sb = load_list("n2_sb", n2)
+        x_byte_table = load_scale_table("x_byte_table", x_scales, "x_byte_table")
         d_word_table = load_word_table("d_word_table", d_words)
         x_word_table = load_word_table("x_word_table", x_words)
         w_raw = sb.tile([P, 2 * S], U8, name="w_raw", align_bytes=64)
         nc.sync.dma_start(w_raw[:].bitcast(I32), w1_words[0].bitcast(I32))
-        w_bytes_raw = load_scale_table("w_bytes_raw", w1_scales)
+        n2_sb = load_list("n2_sb", n2)
         n3_sb = load_list("n3_sb", n3)
         n4_sb = load_list("n4_sb", n4)
 
-        gn_sb = sb.tile([P, PACK], F32, name="gn_sb")
-        nc.gpsimd.dma_start(gn_sb[:], gn.rearrange("(p t) o -> p (t o)", t=PACK))
         key_weight = sb.tile([P, PACK], F32, name="key_weight")
         nc.scalar.activation(key_weight[:], gn_sb[:], COPY, scale=Z_FACTOR)
 
         d_bytes_picked = sb.tile([P, S], U8, name="d_bytes_picked", align_bytes=64)
-        x_bytes_picked = sb.tile([P, S], U8, name="x_bytes_picked", align_bytes=64)
+        x_bytes_picked = sb.tile([P, S], U8, name="x_bytes_picked", tag="x_bytes_picked", align_bytes=64)
         planes = sb.tile([P, 2 * S], U8, name="planes", align_bytes=64)
         nc.vector.tensor_copy(d_bytes_picked[:], d_byte_table[:].indirect(kidx_sb[:]))
         nc.vector.tensor_copy(x_bytes_picked[:], x_byte_table[:].indirect(offs_sb[:]))
@@ -92,6 +92,10 @@ def tile_picked_keyquadbond_none_po_kernel(
         for a in range(2):
             nc.vector.tensor_copy(x_picked[a][:].bitcast(U32), x_word_table[:].bitcast(U32).indirect(offs_sb[:, 16 * a : 16 * a + 16]))
 
+        w_bytes_raw = sb.tile([P, S], U8, name="w_bytes_raw", tag="x_bytes_picked", align_bytes=64)
+        nc.gpsimd.memset(w_bytes_raw[:].bitcast(I32), 0)
+        for q in range(4):
+            nc.sync.dma_start(w_bytes_raw[32 * q : 32 * q + 4, :].bitcast(I32), w1_scales[0, 4 * q : 4 * q + 4, :].bitcast(I32))
         w_dealt = sb.tile([P, 2 * S], U8, name="w_dealt", align_bytes=64)
         w_plane = sb.tile([P, S], U8, name="w_plane", align_bytes=64)
         nc.vector.tensor_copy(
@@ -100,8 +104,6 @@ def tile_picked_keyquadbond_none_po_kernel(
         nc.vector.tensor_copy(
             w_plane[:].rearrange("p (t m) -> p t m", t=PACK), w_bytes_raw[:].rearrange("p (m t) -> p t m", t=PACK)
         )
-        for r in range(1, 4):
-            nc.sync.dma_start(w_plane[r:P:32, :].bitcast(I32), w_plane[8 * r : P : 32, :].bitcast(I32))
 
         banks = [ps.tile([P, S], F32, name="bank%d" % b) for b in range(8)]
         window = [sb.tile([P, S if t == 0 else 2 * S], F32, name="window%d" % t) for t in range(PACK)]
@@ -180,7 +182,7 @@ def tile_picked_keyquadbond_none_po_kernel(
         values(0, chunks[1], banks[1])
         quantise_z(chunks[2])
         values(0, chunks[2], banks[2])
-        for t in range(1, PACK):
+        for t in (2, 1, 3):
             values(t, slice(0, S), banks[2 + t])
 
         pa = [sb.tile([P, HALF], F32, name="pa%d" % t) for t in range(PACK)]
@@ -204,19 +206,31 @@ def tile_picked_keyquadbond_none_po_kernel(
             nc.vector.tensor_tensor(y[t][:].indirect(n4_sb[:]), pa[t][:], pb[t][:], ALU.mult)
             nc.sync.dma_start(out_rows[:, t, :], y[t][:])
 
+        def round_plane(t):
+            if t == 2:
+                nc.scalar.copy(y_grouped[:, :, 2:4], y[t][:].unsqueeze(2).to_broadcast([P, S, 2]))
+            else:
+                nc.scalar.copy(y_grouped[:, :, t], y[t][:])
+
         fetch_a(0)
         fetch_b(0)
-        for t in range(PACK):
-            if t + 1 < PACK:
-                fetch_a(t + 1)
-            put_sum(t)
-            if t + 1 < PACK:
-                fetch_b(t + 1)
-            put_product(t)
-            if t < 2:
-                nc.scalar.copy(y_grouped[:, :, t], y[t][:])
-            elif t == 2:
-                nc.scalar.copy(y_grouped[:, :, 2:4], y[t][:].unsqueeze(2).to_broadcast([P, S, 2]))
+        fetch_a(2)
+        put_sum(0)
+        fetch_b(2)
+        put_product(0)
+        round_plane(0)
+        fetch_a(1)
+        put_sum(2)
+        fetch_b(1)
+        put_product(2)
+        round_plane(2)
+        fetch_a(3)
+        fetch_b(3)
+        put_sum(1)
+        put_sum(3)
+        put_product(1)
+        round_plane(1)
+        put_product(3)
         nc.vector.tensor_copy(y_grouped[:, :256, 3], y[3][:, :256])
         nc.vector.tensor_copy(y_grouped[:, 256:384, 3], y[3][:, 256:384])
         nc.scalar.copy(y_grouped[:, 384:, 3], y[3][:, 384:])

@@ -37,10 +37,10 @@ def tile_picked_keyquadbond_none_po_kernel(
             nc.sync.dma_start(t[:], dram)
             return t
 
-        def load_scale_table(name, dram, tag):
+        def load_scale_table(name, dram, clear):
             width = dram.shape[2]
-            t = sb.tile([P, width], U8, name=name, tag=tag, align_bytes=64)
-            nc.gpsimd.memset(t[:].bitcast(I32), 0)
+            t = sb.tile([P, width], U8, name=name, align_bytes=64)
+            clear.memset(t[:].bitcast(I32), 0)
             nc.sync.dma_start(t[0:P:8, :].bitcast(I32), dram[0].bitcast(I32))
             return t
 
@@ -50,18 +50,17 @@ def tile_picked_keyquadbond_none_po_kernel(
             return t
 
         kidx_sb = load_list("kidx_sb", kidx)
-        d_byte_table = sb.tile([P, TABLE], U8, name="d_byte_table", align_bytes=64)
-        nc.sync.dma_start(d_byte_table[:].bitcast(I32), d_scales[0].bitcast(I32).unsqueeze(1).to_broadcast([16, 8, TABLE // 4]))
         offs_sb = load_list("offs_sb", offs)
         gn_sb = sb.tile([P, PACK], F32, name="gn_sb")
         nc.sync.dma_start(gn_sb[:], gn.rearrange("(p t) o -> p (t o)", t=PACK))
         n1_sb = load_list("n1_sb", n1)
-        x_byte_table = load_scale_table("x_byte_table", x_scales, "x_byte_table")
+        n2_sb = load_list("n2_sb", n2)
+        d_byte_table = load_scale_table("d_byte_table", d_scales, nc.gpsimd)
+        x_byte_table = load_scale_table("x_byte_table", x_scales, nc.vector)
         d_word_table = load_word_table("d_word_table", d_words)
         x_word_table = load_word_table("x_word_table", x_words)
         w_raw = sb.tile([P, 2 * S], U8, name="w_raw", align_bytes=64)
         nc.sync.dma_start(w_raw[:].bitcast(I32), w1_words[0].bitcast(I32))
-        n2_sb = load_list("n2_sb", n2)
         n3_sb = load_list("n3_sb", n3)
         n4_sb = load_list("n4_sb", n4)
 
@@ -96,22 +95,23 @@ def tile_picked_keyquadbond_none_po_kernel(
         nc.gpsimd.memset(w_bytes_raw[:].bitcast(I32), 0)
         for q in range(4):
             nc.sync.dma_start(w_bytes_raw[32 * q : 32 * q + 4, :].bitcast(I32), w1_scales[0, 4 * q : 4 * q + 4, :].bitcast(I32))
-        w_dealt = sb.tile([P, 2 * S], U8, name="w_dealt", align_bytes=64)
-        w_plane = sb.tile([P, S], U8, name="w_plane", align_bytes=64)
-        nc.vector.tensor_copy(
-            w_dealt[:].rearrange("p (t m b) -> p t m b", t=PACK, b=2), w_raw[:].rearrange("p (m t b) -> p t m b", t=PACK, b=2)
-        )
-        nc.vector.tensor_copy(
-            w_plane[:].rearrange("p (t m) -> p t m", t=PACK), w_bytes_raw[:].rearrange("p (m t) -> p t m", t=PACK)
-        )
+        def deal_w(name, tiles, word_tag, byte_tag):
+            count = 2
+            words = sb.tile([P, count, P, 2], U8, name=name + "_words", tag=word_tag, align_bytes=64)
+            plane = sb.tile([P, count, P], U8, name=name + "_plane", tag=byte_tag, align_bytes=64)
+            nc.vector.tensor_copy(words[:], w_raw[:].rearrange("p (m t b) -> p t m b", t=PACK, b=2)[:, tiles])
+            nc.vector.tensor_copy(plane[:], w_bytes_raw[:].rearrange("p (m t) -> p t m", t=PACK)[:, tiles])
+            return {tiles.start + 2 * i: (words[:, i].rearrange("p m b -> p (m b)"), plane[:, i]) for i in range(count)}
+
+        w_tiles = deal_w("w_first", slice(0, PACK, 2), "w_first_words", "w_first_plane")
 
         banks = [ps.tile([P, S], F32, name="bank%d" % b) for b in range(8)]
         window = [sb.tile([P, S if t == 0 else 2 * S], F32, name="window%d" % t) for t in range(PACK)]
         last_plain = sb.tile([P, S], F32, name="last_plain")
         plain = [window[t + 1][:, S:] for t in range(PACK - 1)] + [last_plain[:]]
         diff1 = sb.tile([P, PACK, S], F32, name="diff1")
-        diff1w = sb.tile([P, PACK, S], F32, name="diff1w")
-        diff2 = sb.tile([P, PACK, S], F32, name="diff2")
+        diff1w = sb.tile([P, PACK, S], F32, name="diff1w", tag="diff1w", align_bytes=64)
+        diff2 = sb.tile([P, PACK, S], F32, name="diff2", tag="diff2", align_bytes=64)
 
         def score(t, a):
             cols = slice(HALF * a, HALF * (a + 1))
@@ -126,7 +126,10 @@ def tile_picked_keyquadbond_none_po_kernel(
                 stop=True,
             )
             nc.scalar.copy(window[t][:, cols], bank)
-            nc.scalar.copy(plain[t][:, cols], bank)
+            if t == 0 and a == 0:
+                nc.vector.tensor_copy(plain[t][:, cols], bank)
+            else:
+                nc.scalar.copy(plain[t][:, cols], bank)
 
         def differences(t, cols):
             lcols = slice(cols.start // 16, cols.stop // 16)
@@ -163,8 +166,8 @@ def tile_picked_keyquadbond_none_po_kernel(
         def values(t, cols, bank):
             nc.tensor.matmul_mx(
                 bank[:, cols],
-                lhsT=w_dealt[:, 2 * P * t : 2 * P * (t + 1)].bitcast(FP4X4),
-                lhsT_scale=w_plane[:, P * t : P * (t + 1)],
+                lhsT=w_tiles[t][0].bitcast(FP4X4),
+                lhsT_scale=w_tiles[t][1],
                 rhs=z_codes[:, cols].bitcast(FP8X4),
                 rhs_scale=z_plane[:, cols],
                 start=True,
@@ -182,7 +185,9 @@ def tile_picked_keyquadbond_none_po_kernel(
         values(0, chunks[1], banks[1])
         quantise_z(chunks[2])
         values(0, chunks[2], banks[2])
-        for t in (2, 1, 3):
+        values(2, slice(0, S), banks[4])
+        w_tiles = deal_w("w_rest", slice(1, PACK, 2), "diff1w", "diff2")
+        for t in (1, 3):
             values(t, slice(0, S), banks[2 + t])
 
         pa = [sb.tile([P, HALF], F32, name="pa%d" % t) for t in range(PACK)]

from contextlib import ExitStack

import concourse.mybir as mybir

FLOPS = 536870912

F32 = mybir.dt.float32
BF16 = mybir.dt.bfloat16
I32 = mybir.dt.int32
U32 = mybir.dt.uint32
U16 = mybir.dt.uint16
U8 = mybir.dt.uint8
FP8X4 = mybir.dt.float8_e4m3fn_x4
FP4X4 = mybir.dt.float4_e2m1fn_x4
ALU = mybir.AluOpType
COPY = mybir.ActivationFunctionType.Copy

P = 128
PACK = 4
TABLE = 2048
S = 512
HALF = S // 2
Z_FACTOR = 0.75 * 0.0625 * 0.0625


def tile_picked_keyquadbond_none_po_kernel(
    tc, x_words, x_scales, d_words, d_scales, gn, w1_words, w1_scales, offs, kidx, n1, n2, n3, n4, out_0, out_1, out_2
):
    nc = tc.nc
    with ExitStack() as ctx:
        lists = ctx.enter_context(tc.tile_pool(name="lists", bufs=1))
        sb = ctx.enter_context(tc.tile_pool(name="sb", bufs=1))
        ps = ctx.enter_context(tc.psum_pool(name="ps", bufs=1))

        def load_list(name, dram):
            t = lists.tile(list(dram.shape), U16, name=name)
            nc.sync.dma_start(t[:], dram)
            return t

        def load_scale_table(name, dram, clear):
            width = dram.shape[2]
            t = sb.tile([P, width], U8, name=name, align_bytes=64)
            clear.memset(t[:].bitcast(I32), 0)
            nc.sync.dma_start(t[0:P:8, :].bitcast(I32), dram[0].bitcast(I32))
            return t

        def load_word_table(name, dram):
            t = sb.tile([P, TABLE], I32, name=name, align_bytes=64)
            nc.sync.dma_start(t[:], dram[0].rearrange("p n t -> p (n t)").bitcast(I32))
            return t

        kidx_sb = load_list("kidx_sb", kidx)
        offs_sb = load_list("offs_sb", offs)
        gn_sb = sb.tile([P, PACK], F32, name="gn_sb")
        nc.sync.dma_start(gn_sb[:], gn.rearrange("(p t) o -> p (t o)", t=PACK))
        n1_sb = load_list("n1_sb", n1)
        n2_sb = load_list("n2_sb", n2)
        d_byte_table = load_scale_table("d_byte_table", d_scales, nc.gpsimd)
        x_byte_table = load_scale_table("x_byte_table", x_scales, nc.vector)
        d_word_table = load_word_table("d_word_table", d_words)
        x_word_table = load_word_table("x_word_table", x_words)
        w_raw = sb.tile([P, 2 * S], U8, name="w_raw", align_bytes=64)
        nc.sync.dma_start(w_raw[:].bitcast(I32), w1_words[0].bitcast(I32))
        n3_sb = load_list("n3_sb", n3)
        n4_sb = load_list("n4_sb", n4)

        key_weight = sb.tile([P, PACK], F32, name="key_weight")
        nc.scalar.activation(key_weight[:], gn_sb[:], COPY, scale=Z_FACTOR)

        d_bytes_picked = sb.tile([P, S], U8, name="d_bytes_picked", align_bytes=64)
        x_bytes_picked = sb.tile([P, S], U8, name="x_bytes_picked", tag="x_bytes_picked", align_bytes=64)
        planes = sb.tile([P, 2 * S], U8, name="planes", align_bytes=64)
        nc.vector.tensor_copy(d_bytes_picked[:], d_byte_table[:].indirect(kidx_sb[:]))
        nc.vector.tensor_copy(x_bytes_picked[:], x_byte_table[:].indirect(offs_sb[:]))
        nc.vector.tensor_copy(
            planes[:, :S].rearrange("p (t m) -> p t m", t=PACK), d_bytes_picked[:].rearrange("p (m t) -> p t m", t=PACK)
        )
        nc.vector.tensor_copy(planes[:, S:].bitcast(I32), x_bytes_picked[:].bitcast(I32))
        for r in range(1, 4):
            nc.scalar.dma_start(planes[r:P:32, :].bitcast(I32), planes[8 * r : P : 32, :].bitcast(I32))
        d_plane = planes[:, :S]
        x_plane = planes[:, S:]

        d_picked = sb.tile([P, S], I32, name="d_picked", align_bytes=64)
        d_dealt = sb.tile([P, S], I32, name="d_dealt", align_bytes=64)
        nc.vector.tensor_copy(d_picked[:].bitcast(U32), d_word_table[:].bitcast(U32).indirect(kidx_sb[:]))
        x_picked = [sb.tile([P, HALF], I32, name="x_picked%d" % a, align_bytes=64) for a in range(2)]
        nc.vector.tensor_copy(
            d_dealt[:].rearrange("p (t m) -> p t m", t=PACK), d_picked[:].rearrange("p (m t) -> p t m", t=PACK)
        )
        for a in range(2):
            nc.vector.tensor_copy(x_picked[a][:].bitcast(U32), x_word_table[:].bitcast(U32).indirect(offs_sb[:, 16 * a : 16 * a + 16]))

        w_bytes_raw = sb.tile([P, S], U8, name="w_bytes_raw", tag="x_bytes_picked", align_bytes=64)
        nc.gpsimd.memset(w_bytes_raw[:].bitcast(I32), 0)
        for q in range(4):
            nc.sync.dma_start(w_bytes_raw[32 * q : 32 * q + 4, :].bitcast(I32), w1_scales[0, 4 * q : 4 * q + 4, :].bitcast(I32))
        def deal_w(name, tiles, word_tag, byte_tag):
            count = 2
            words = sb.tile([P, count, P, 2], U8, name=name + "_words", tag=word_tag, align_bytes=64)
            plane = sb.tile([P, count, P], U8, name=name + "_plane", tag=byte_tag, align_bytes=64)
            nc.vector.tensor_copy(words[:], w_raw[:].rearrange("p (m t b) -> p t m b", t=PACK, b=2)[:, tiles])
            nc.vector.tensor_copy(plane[:], w_bytes_raw[:].rearrange("p (m t) -> p t m", t=PACK)[:, tiles])
            return {tiles.start + 2 * i: (words[:, i].rearrange("p m b -> p (m b)"), plane[:, i]) for i in range(count)}

        w_tiles = deal_w("w_first", slice(0, PACK, 2), "w_first_words", "w_first_plane")

        banks = [ps.tile([P, S], F32, name="bank%d" % b) for b in range(8)]
        window = [sb.tile([P, S if t == 0 else 2 * S], F32, name="window%d" % t) for t in range(PACK)]
        last_plain = sb.tile([P, S], F32, name="last_plain")
        plain = [window[t + 1][:, S:] for t in range(PACK - 1)] + [last_plain[:]]
        diff1 = sb.tile([P, PACK, S], F32, name="diff1")
        diff1w = sb.tile([P, PACK, S], F32, name="diff1w", tag="diff1w", align_bytes=64)
        diff2 = sb.tile([P, PACK, S], F32, name="diff2", tag="diff2", align_bytes=64)

        def score(t, a):
            cols = slice(HALF * a, HALF * (a + 1))
            bank = banks[2 * t + a][:, :HALF]
            nc.tensor.matmul_mx(
                bank,
                lhsT=d_dealt[:, P * t : P * (t + 1)].bitcast(FP8X4),
                lhsT_scale=d_plane[:, P * t : P * (t + 1)],
                rhs=x_picked[a][:].bitcast(FP8X4),
                rhs_scale=x_plane[:, cols],
                start=True,
                stop=True,
            )
            nc.scalar.copy(window[t][:, cols], bank)
            if t == 0 and a == 0:
                nc.vector.tensor_copy(plain[t][:, cols], bank)
            else:
                nc.scalar.copy(plain[t][:, cols], bank)

        def differences(t, cols):
            lcols = slice(cols.start // 16, cols.stop // 16)
            nc.vector.tensor_tensor(diff1[:, t, cols], window[t][:].indirect(n1_sb[:, lcols]), plain[t][:, cols], ALU.subtract)
            nc.vector.tensor_tensor(diff2[:, t, cols], window[t][:].indirect(n2_sb[:, lcols]), plain[t][:, cols], ALU.subtract)

        for t in range(PACK):
            score(t, 0)
            score(t, 1)
        for t in range(PACK):
            if t == 0:
                differences(t, slice(0, HALF))
                differences(t, slice(HALF, S))
            else:
                differences(t, slice(0, S))
            nc.scalar.activation(diff1w[:, t, :], diff1[:, t, :], COPY, scale=key_weight[:, t : t + 1])

        z = sb.tile([P, S, PACK], BF16, name="z", align_bytes=64)
        z_codes = sb.tile([P, S], U32, name="z_codes", align_bytes=64)
        z_plane = sb.tile([P, S], U8, name="z_plane", align_bytes=64)
        h = [sb.tile([P, S], F32, name="h%d" % t) for t in range(PACK)]

        def product(cols):
            nc.vector.tensor_tensor(
                z[:, cols, :].rearrange("p (c i) t -> p c t i", i=4),
                diff1w[:, :, cols].rearrange("p t (c i) -> p c t i", i=4),
                diff2[:, :, cols].rearrange("p t (c i) -> p c t i", i=4),
                ALU.mult,
            )

        def quantise_z(cols):
            nc.vector.quantize_mx(z_codes[:, cols].bitcast(FP8X4), z_plane[:, cols], z[:, cols, :].rearrange("p c t -> p (c t)"))

        def values(t, cols, bank):
            nc.tensor.matmul_mx(
                bank[:, cols],
                lhsT=w_tiles[t][0].bitcast(FP4X4),
                lhsT_scale=w_tiles[t][1],
                rhs=z_codes[:, cols].bitcast(FP8X4),
                rhs_scale=z_plane[:, cols],
                start=True,
                stop=True,
            )
            nc.scalar.copy(h[t][:, cols], bank[:, cols])

        chunks = [slice(0, 256), slice(256, 384), slice(384, 512)]
        product(chunks[0])
        product(chunks[1])
        quantise_z(chunks[0])
        values(0, chunks[0], banks[0])
        product(chunks[2])
        quantise_z(chunks[1])
        values(0, chunks[1], banks[1])
        quantise_z(chunks[2])
        values(0, chunks[2], banks[2])
        values(2, slice(0, S), banks[4])
        w_tiles = deal_w("w_rest", slice(1, PACK, 2), "diff1w", "diff2")
        for t in (1, 3):
            values(t, slice(0, S), banks[2 + t])

        pa = [sb.tile([P, HALF], F32, name="pa%d" % t) for t in range(PACK)]
        pb = [sb.tile([P, HALF], F32, name="pb%d" % t) for t in range(PACK)]
        y = [sb.tile([P, S], F32, name="y%d" % t) for t in range(PACK)]
        y_grouped = sb.tile([P, S, PACK], BF16, name="y_grouped", align_bytes=64)
        y_codes = sb.tile([P, S], I32, name="y_codes", align_bytes=64)
        y_plane = sb.tile([P, S], U8, name="y_plane", align_bytes=64)
        out_rows = out_0.rearrange("(p t) j -> p t j", t=PACK)

        def fetch_a(t):
            nc.vector.tensor_copy(pa[t][:], h[t][:].indirect(n3_sb[:]))

        def fetch_b(t):
            nc.vector.tensor_copy(pb[t][:], h[t][:].indirect(n4_sb[:]))

        def put_sum(t):
            nc.vector.tensor_tensor(y[t][:].indirect(n3_sb[:]), pa[t][:], pb[t][:], ALU.add)

        def put_product(t):
            nc.vector.tensor_tensor(y[t][:].indirect(n4_sb[:]), pa[t][:], pb[t][:], ALU.mult)
            nc.sync.dma_start(out_rows[:, t, :], y[t][:])

        def round_plane(t):
            if t == 2:
                nc.scalar.copy(y_grouped[:, :, 2:4], y[t][:].unsqueeze(2).to_broadcast([P, S, 2]))
            else:
                nc.scalar.copy(y_grouped[:, :, t], y[t][:])

        fetch_a(0)
        fetch_b(0)
        fetch_a(2)
        put_sum(0)
        fetch_b(2)
        put_product(0)
        round_plane(0)
        fetch_a(1)
        put_sum(2)
        fetch_b(1)
        put_product(2)
        round_plane(2)
        fetch_a(3)
        fetch_b(3)
        put_sum(1)
        put_sum(3)
        put_product(1)
        round_plane(1)
        put_product(3)
        nc.vector.tensor_copy(y_grouped[:, :256, 3], y[3][:, :256])
        nc.vector.tensor_copy(y_grouped[:, 256:384, 3], y[3][:, 256:384])
        nc.scalar.copy(y_grouped[:, 384:, 3], y[3][:, 384:])
        words_out = out_1[0].rearrange("p n t -> p (n t)").bitcast(I32)
        for a in range(2):
            cols = slice(HALF * a, HALF * (a + 1))
            nc.vector.quantize_mx(y_codes[:, cols].bitcast(FP8X4), y_plane[:, cols], y_grouped[:, cols, :].rearrange("p c t -> p (c t)"))
            queue = nc.sync if a == 0 else nc.scalar
            queue.dma_start(words_out[:, cols], y_codes[:, cols])
        for q in range(4):
            queue = nc.sync if q % 2 == 0 else nc.scalar
            queue.dma_start(out_2[0, 4 * q : 4 * q + 4, :].bitcast(I32), y_plane[32 * q : 32 * q + 4, :].bitcast(I32))
